import numpy as np
import ml_dtypes


def mxq(x, axis, fmt="e4m3"):
    dtype, down = {"e4m3": (ml_dtypes.float8_e4m3fn, 7), "e5m2": (ml_dtypes.float8_e5m2, 14)}[fmt]
    v = np.moveaxis(np.asarray(x, np.float32).astype(ml_dtypes.bfloat16).astype(np.float64), axis, -1)
    blocks = v.reshape(v.shape[:-1] + (-1, 32))
    amax = np.abs(blocks).max(-1, keepdims=True)
    byte = np.maximum(np.where(amax > 0, np.frexp(amax)[1] - 1 + 127, 0) - down, 1)
    scale = np.exp2(byte - 127.0)
    codes = (blocks / scale).astype(np.float32).astype(dtype).astype(np.float64)
    return np.moveaxis((codes * scale).reshape(v.shape), -1, axis)


WIDE = False


def mx_kscale(k):
    if not WIDE:
        return np.ones(k)
    levels = np.array([10, -10, 5, -5, 0])
    if k % 512:
        return np.exp2(np.random.permutation(np.resize(levels, k // 32))).repeat(32)
    a = np.empty((k // 512, 16))
    for p in range(k // 512):
        a[p, :8] = np.random.permutation(np.resize(levels, 8))
        for g in range(8):
            far = levels[np.abs(levels - a[p, g]) >= 10]
            a[p, g + 8] = far[np.random.randint(len(far))]
    return np.exp2(a.ravel()).repeat(32)


def f64(x):
    return np.asarray(x).astype(np.float64)


def striped(idx):
    return np.tile(idx.reshape(-1, 16).T, (8, 1)).astype(np.uint16)


def unstriped(offs):
    return offs[:16].T.reshape(-1).astype(np.int64)


def pack_weight(w):
    k, n = w.shape
    w = f64(np.asarray(w, np.float32).astype(ml_dtypes.bfloat16)).reshape(k // 32, 32, n)
    amax = np.abs(w).max(1)
    byte = np.clip(np.where(amax > 0, np.frexp(amax)[1] - 1 + 127 - 7, 1), 1, 254)
    scaled = (w * np.exp2(127.0 - byte)[:, None, :]).reshape(k, n).astype(np.float32)
    words = np.ascontiguousarray(scaled.reshape(k // 512, 128, 4, n).transpose(0, 1, 3, 2)).astype(ml_dtypes.float8_e4m3fn).view(np.uint8)
    return words, np.ascontiguousarray(byte.astype(np.uint8).reshape(k // 512, 16, n))


def unpack_weight(words, scales):
    g, p, n, _ = words.shape
    vals = np.ascontiguousarray(words).view(ml_dtypes.float8_e4m3fn).astype(np.float64) * np.repeat(np.exp2(scales.astype(np.float64) - 127.0), 8, axis=1)[..., None]
    return vals.transpose(0, 1, 3, 2).reshape(g * 512, n)


K, T, S, N, H = 1024, 1024, 512, 256, 512


def setup_inputs():
    n = np.random.standard_normal
    s = mx_kscale(K)[:, None]
    u = mx_kscale(H)
    packed_xT = pack_weight(n((K, T)) * s)
    return {
        "x_words": packed_xT[0],
        "x_scales": packed_xT[1],
        "w1": (n((K, H)) / np.sqrt(K) / s).astype(np.float32),
        "w2": (n((K, H)) / np.sqrt(K) / s).astype(np.float32),
        "eps": (np.random.uniform(0.3, 2.0, (H, S))).astype(np.float32),
        "unit": (np.random.uniform(0.6, 1.4, (H, 1)) * u[:, None]).astype(np.float32),
        "w3": (n((H, N)) / np.sqrt(H) / u[:, None]).astype(np.float32),
        "offs": striped(np.random.permutation(T)[:S]),
        "prv": striped(np.random.permutation(S)),
    }


def reference(x_words, x_scales, w1, w2, eps, unit, w3, offs, prv):
    xq = unpack_weight(x_words, x_scales)[:, unstriped(offs)]
    vo = mxq(f64(w2), 0, "e4m3").T @ xq
    y = mxq(f64(w1), 0, "e4m3").T @ xq
    psi = 0.8 * (np.log(np.exp(y) + 1.0)) + 0.2
    pp = psi[:, unstriped(prv)]
    dur = pp * f64(eps)
    psin = 0.3 * dur + 0.5 * psi + 0.1
    haz = np.sqrt(dur) / psin
    volu = (np.log(np.exp(vo) + 1.0)) * (haz / (haz + 0.7))
    hid = f64(unit) * (volu - (0.5 * np.log(psin)))
    return mxq(f64(w3), 0, "e4m3").T @ mxq(hid, 0, "e4m3")

@@ -1,0 +1,266 @@
+import math
+from contextlib import ExitStack
+
+import concourse.mybir as mybir
+from concourse.masks import make_identity
+
+K, T, S, N, H = 1024, 1024, 512, 256, 512
+FLOPS = 2 * K * H * S * 2 + 2 * H * N * S
+
+F32 = mybir.dt.float32
+BF16 = mybir.dt.bfloat16
+I32 = mybir.dt.int32
+U32 = mybir.dt.uint32
+U16 = mybir.dt.uint16
+U8 = mybir.dt.uint8
+FP8X4 = mybir.dt.float8_e4m3fn_x4
+ALU = mybir.AluOpType
+ACT = mybir.ActivationFunctionType
+
+P = 128
+PACK = 4
+K_PASS = P * PACK
+PASSES = K // K_PASS
+TINY = 2.0 ** -60
+CHUNKS = S // P
+HALF = S // 2
+
+
+def tile_picked_yacddu_vol_p_kernel(
+    tc, x_words, x_scales, w1, w2, eps, unit, w3, offs, prv, out
+):
+    nc = tc.nc
+    with ExitStack() as ctx:
+        keep = ctx.enter_context(tc.tile_pool(name="keep", bufs=1))
+        psum = ctx.enter_context(tc.psum_pool(name="psum", bufs=1))
+
+        def sb(name, shape, dtype):
+            return keep.tile(shape, dtype, name=name, align_bytes=64)
+
+        offs_sb = keep.tile([P, S // 16], U16, name="offs_sb")
+        prv_sb = keep.tile([P, S // 16], U16, name="prv_sb")
+        xw = [sb("xw%d" % o, [P, T], U32) for o in range(PASSES)]
+        xs = sb("xs", [P, T], U8)
+        raw = {}
+        for name in ("w1", "w2"):
+            for o in range(PASSES):
+                for half in range(2):
+                    raw[name, o, half] = sb("raw_%s_%d_%d" % (name, o, half), [P, PACK, H // 2], F32)
+        raw3 = sb("raw3", [P, PACK, N], F32)
+        eps_sb = sb("eps_sb", [P, PACK, S], F32)
+        unit_sb = sb("unit_sb", [P, PACK], F32)
+        neg_s = [sb("neg_s%d" % t, [P, S], F32) for t in range(PACK)]
+
+        nc.gpsimd.memset(xs[:].bitcast(I32), 0)
+        ident = sb("ident", [P, P], F32)
+        make_identity(nc, ident[:])
+
+        def load_words(o):
+            nc.sync.dma_start(
+                out=xw[o][:].bitcast(I32),
+                in_=x_words[o].rearrange("p n t -> p (n t)").bitcast(I32),
+            )
+
+        def load_weight(name, w, o):
+            rows = w[o * K_PASS : (o + 1) * K_PASS, :].rearrange("(p j) c -> p j c", j=PACK)
+            for half in range(2):
+                nc.sync.dma_start(
+                    out=raw[name, o, half][:], in_=rows[:, :, half * (H // 2) : (half + 1) * (H // 2)]
+                )
+
+        load_words(0)
+        nc.sync.dma_start(offs_sb[:], offs)
+        for q in range(4):
+            nc.sync.dma_start(
+                out=xs[32 * q : 32 * q + 4 * PASSES, :].bitcast(I32),
+                in_=x_scales[:, 4 * q : 4 * q + 4, :].bitcast(I32),
+            )
+        load_weight("w1", w1, 0)
+        load_words(1)
+        load_weight("w1", w1, 1)
+        load_weight("w2", w2, 0)
+        load_weight("w2", w2, 1)
+        nc.sync.dma_start(out=raw3[:], in_=w3.rearrange("(p j) n -> p j n", j=PACK))
+        nc.sync.dma_start(out=eps_sb[:], in_=eps.rearrange("(p t) s -> p t s", t=PACK))
+        nc.sync.dma_start(prv_sb[:], prv)
+        nc.sync.dma_start(out=unit_sb[:], in_=unit.rearrange("(p t) o -> p (t o)", t=PACK))
+
+        xg = [sb("xg%d" % o, [P, S], U32) for o in range(PASSES)]
+        xsg = sb("xsg", [P, S], U8)
+
+        def gather_words(o):
+            nc.vector.tensor_copy(xg[o][:], xw[o][:].indirect(offs_sb[:]))
+
+        def deal_weight(name, o, sign):
+            grouped = sb("grp_%s_%d" % (name, o), [P, PACK * P * PACK], BF16)
+            view = grouped[:].rearrange("p (t m j) -> p m j t", t=PACK, j=PACK)
+            for half in range(2):
+                src = raw[name, o, half][:].rearrange("p j (m t) -> p m j t", t=PACK)
+                dst = view[:, half * (P // 2) : (half + 1) * (P // 2)]
+                nc.vector.tensor_scalar(dst, src, sign, None, ALU.mult)
+            return grouped
+
+        def quantise_weight(name, o, grouped, pieces):
+            codes = sb("codes_%s_%d" % (name, o), [P, H], U32)
+            scales = sb("scales_%s_%d" % (name, o), [P, H], U8)
+            w = H // pieces
+            for i in range(pieces):
+                nc.vector.quantize_mx(
+                    out=codes[:, i * w : (i + 1) * w].bitcast(FP8X4),
+                    scales=scales[:, i * w : (i + 1) * w],
+                    in_=grouped[:, PACK * i * w : PACK * (i + 1) * w],
+                )
+            return codes, scales
+
+        def product_pass(banks, o, codes, scales):
+            for t in range(PACK):
+                cols = slice(t * P, (t + 1) * P)
+                nc.tensor.matmul_mx(
+                    out=banks[t][:],
+                    lhsT=codes[:, cols].bitcast(FP8X4),
+                    lhsT_scale=scales[:, cols],
+                    rhs=xg[o][:].bitcast(FP8X4),
+                    rhs_scale=xsg[4 * o : P, :],
+                    start=(o == 0),
+                    stop=(o == PASSES - 1),
+                )
+
+        neg_y = [psum.tile([P, S], F32, name="neg_y%d" % t, tag="bank%d" % t) for t in range(PACK)]
+        vo = [psum.tile([P, S], F32, name="vo%d" % t, tag="bank%d" % (PACK + t)) for t in range(PACK)]
+
+        gather_words(0)
+        nc.vector.tensor_copy(xsg[:], xs[:].indirect(offs_sb[:]))
+        c, s = quantise_weight("w1", 0, deal_weight("w1", 0, -1.0), 1)
+        product_pass(neg_y, 0, c, s)
+        gather_words(1)
+        c, s = quantise_weight("w1", 1, deal_weight("w1", 1, -1.0), PACK)
+        product_pass(neg_y, 1, c, s)
+
+        sig_y = sb("sig_y", [P, PACK, S], F32)
+        for t in range(PACK):
+            nc.scalar.activation(sig_y[:, t, :], neg_y[t][:], ACT.Sigmoid)
+        log_y = sb("log_y", [P, PACK, S], F32)
+        nc.scalar.activation(log_y[:], sig_y[:], ACT.Ln, bias=TINY, scale=math.exp(-0.25))
+
+        for o in range(PASSES):
+            c, s = quantise_weight("w2", o, deal_weight("w2", o, 1.0), 1)
+            for ch in range(CHUNKS):
+                cols = slice(ch * P, (ch + 1) * P)
+                nc.tensor.matmul_mx(
+                    out=vo[ch][:],
+                    lhsT=xg[o][:, cols].bitcast(FP8X4),
+                    lhsT_scale=xsg[4 * o : P, cols],
+                    rhs=c[:].bitcast(FP8X4),
+                    rhs_scale=s[:],
+                    start=(o == 0),
+                    stop=(o == PASSES - 1),
+                )
+
+        grp3 = sb("grp3", [P, N * PACK], BF16)
+        nc.vector.tensor_copy(
+            out=grp3[:].rearrange("p (c i j) -> p c j i", i=4, j=PACK),
+            in_=raw3[:].rearrange("p j (c i) -> p c j i", i=4),
+        )
+        codes3 = sb("codes3", [P, N], U32)
+        scales3 = sb("scales3", [P, N], U8)
+        nc.vector.quantize_mx(out=codes3[:].bitcast(FP8X4), scales=scales3[:], in_=grp3[:])
+
+        for t in range(PACK):
+            nc.gpsimd.tensor_scalar(eps_sb[:, t, :], eps_sb[:, t, :], 0.6, 0.0, ALU.mult, ALU.add)
+
+        sig_v = sb("sig_v", [P, CHUNKS, H], F32)
+        for ch in range(CHUNKS):
+            nc.scalar.activation(sig_v[:, ch, :], vo[ch][:], ACT.Sigmoid, scale=-1.0)
+        log_v = sb("log_v", [P, CHUNKS, H], F32)
+        nc.scalar.activation(log_v[:], sig_v[:], ACT.Ln, bias=TINY)
+
+        for t in range(PACK):
+            nc.vector.scalar_tensor_tensor(
+                neg_s[t][:], neg_y[t][:], -0.25, log_y[:, t, :], ALU.add, ALU.min
+            )
+        neg_d = [sb("neg_d%d" % h, [P, PACK, HALF], F32) for h in range(2)]
+        for h in range(2):
+            for t in range(PACK):
+                nc.vector.tensor_tensor(
+                    neg_d[h][:, t, :],
+                    neg_s[t][:].indirect(prv_sb[:, h * (HALF // 16) : (h + 1) * (HALF // 16)]),
+                    eps_sb[:, t, h * HALF : (h + 1) * HALF],
+                    ALU.mult,
+                )
+
+        def turn(dst, src, start, stop):
+            nc.tensor.matmul(dst, lhsT=src, rhs=ident[:], is_transpose=True, start=start, stop=stop)
+
+        log_dur = sig_v
+        log_psin = sb("log_psin", [P, CHUNKS, H], F32)
+        for ch in range(CHUNKS):
+            cols = slice(ch * P, (ch + 1) * P)
+            h, within = divmod(ch, 2)
+            part = slice(within * P, (within + 1) * P)
+            dur_t = psum.tile([P, PACK, P], F32, name="dur_t%d" % ch, tag="bank%d" % (2 * within))
+            psin_t = psum.tile([P, PACK, P], F32, name="psin_t%d" % ch, tag="bank%d" % (2 * within + 1))
+            for t in range(PACK):
+                turn(psin_t[:, t, :], neg_s[t][:, cols], t == 0, False)
+            for t in range(PACK):
+                turn(dur_t[:, t, :], neg_d[h][:, t, part], True, True)
+            for t in range(PACK):
+                turn(psin_t[:, t, :], neg_d[h][:, t, part], False, t == PACK - 1)
+            nc.scalar.activation(
+                log_dur[:, ch, :], dur_t[:].rearrange("p t c -> p (t c)"), ACT.Ln, bias=TINY, scale=-0.8 / 0.6
+            )
+            nc.scalar.activation(
+                log_psin[:, ch, :], psin_t[:].rearrange("p t c -> p (t c)"), ACT.Ln, bias=0.1, scale=-0.4
+            )
+
+        neg_sp = sb("neg_sp", [P, CHUNKS, H], F32)
+        for ch in range(CHUNKS):
+            nc.vector.scalar_tensor_tensor(
+                neg_sp[:, ch, :], vo[ch][:], -1.0, log_v[:, ch, :], ALU.mult, ALU.min
+            )
+        log_haz = sb("log_haz", [P, CHUNKS, H], F32)
+        for chs in (slice(0, 1), slice(1, 2), slice(2, 4)):
+            nc.vector.scalar_tensor_tensor(
+                log_haz[:, chs, :], log_dur[:, chs, :], 0.5, log_psin[:, chs, :], ALU.mult, ALU.subtract
+            )
+        half_unit = sb("half_unit", [P, PACK], F32)
+        nc.vector.tensor_scalar(half_unit[:], unit_sb[:], -0.5, None, ALU.mult)
+
+        out_view = out.rearrange("(a p) s -> p a s", p=P)
+        ratio = [log_dur[:, (ch + 2) % CHUNKS, :] for ch in range(CHUNKS)]
+        for ch in range(CHUNKS):
+            nc.scalar.activation(ratio[ch], log_haz[:, ch, :], ACT.Sigmoid, bias=-math.log(0.7))
+        for ch in range(CHUNKS):
+            cols = slice(ch * P, (ch + 1) * P)
+            neg_vol = sb("neg_vol%d" % ch, [P, H], F32)
+            nc.vector.scalar_tensor_tensor(
+                neg_vol[:], neg_sp[:, ch, :], 2.0, ratio[ch], ALU.mult, ALU.mult
+            )
+            total = psum.tile([P, PACK, P], F32, name="total%d" % ch, tag="bank%d" % (PACK + ch))
+            for t in range(PACK):
+                turn(total[:, t, :], log_psin[:, ch, t * P : (t + 1) * P], t == 0, False)
+            for t in range(PACK):
+                turn(total[:, t, :], neg_vol[:, t * P : (t + 1) * P], False, t == PACK - 1)
+            hid_grp = sb("hid_grp%d" % ch, [P, P * PACK], BF16)
+            nc.vector.tensor_tensor(
+                hid_grp[:].rearrange("p (c t) -> p c t", t=PACK),
+                total[:].rearrange("p t c -> p c t"),
+                half_unit[:].unsqueeze(1).to_broadcast([P, P, PACK]),
+                ALU.mult,
+            )
+            hid_codes = sb("hid_codes%d" % ch, [P, P], U32)
+            hid_scales = sb("hid_scales%d" % ch, [P, P], U8)
+            nc.vector.quantize_mx(out=hid_codes[:].bitcast(FP8X4), scales=hid_scales[:], in_=hid_grp[:])
+            acc = psum.tile([P, N // P, P], F32, name="acc%d" % ch, tag="bank%d" % ch)
+            for a in range(N // P):
+                nc.tensor.matmul_mx(
+                    out=acc[:, a, :],
+                    lhsT=codes3[:, a * P : (a + 1) * P].bitcast(FP8X4),
+                    lhsT_scale=scales3[:, a * P : (a + 1) * P],
+                    rhs=hid_codes[:].bitcast(FP8X4),
+                    rhs_scale=hid_scales[:],
+                    start=True,
+                    stop=True,
+                )
+            res = sb("res%d" % ch, [P, N // P, P], F32)
+            nc.scalar.copy(out=res[:], in_=acc[:])
+            nc.sync.dma_start(out=out_view[:, :, cols], in_=res[:])

@@ -24,6 +24,7 @@ PASSES = K // K_PASS
 TINY = 2.0 ** -60
 CHUNKS = S // P
 HALF = S // 2
+ON_SCALAR = (0, 2)
 
 
 def tile_picked_yacddu_vol_p_kernel(
@@ -40,18 +41,22 @@ def tile_picked_yacddu_vol_p_kernel(
         offs_sb = keep.tile([P, S // 16], U16, name="offs_sb")
         prv_sb = keep.tile([P, S // 16], U16, name="prv_sb")
         xw = [sb("xw%d" % o, [P, T], U32) for o in range(PASSES)]
+        xs_rows = sb("xs_rows", [P, T], U8)
         xs = sb("xs", [P, T], U8)
         raw = {}
-        for name in ("w1", "w2"):
-            for o in range(PASSES):
-                for half in range(2):
-                    raw[name, o, half] = sb("raw_%s_%d_%d" % (name, o, half), [P, PACK, H // 2], F32)
+        for o in range(PASSES):
+            for half in range(2):
+                raw["w1", o, half] = sb("raw_w1_%d_%d" % (o, half), [P, PACK, H // 2], F32)
+            raw["w2", o] = sb("raw_w2_%d" % o, [P, PACK, H], F32)
         raw3 = sb("raw3", [P, PACK, N], F32)
         eps_sb = sb("eps_sb", [P, PACK, S], F32)
         unit_sb = sb("unit_sb", [P, PACK], F32)
         neg_s = [sb("neg_s%d" % t, [P, S], F32) for t in range(PACK)]
 
-        nc.gpsimd.memset(xs[:].bitcast(I32), 0)
+        nc.vector.memset(xs[:].bitcast(I32), 0)
+        warm = sb("warm", [P, 2], F32)
+        nc.gpsimd.memset(warm[:, 0:1], 0.0)
+        nc.scalar.activation(warm[:, 1:2], warm[:, 0:1], ACT.Sigmoid)
         ident = sb("ident", [P, P], F32)
         make_identity(nc, ident[:])
 
@@ -61,29 +66,37 @@ def tile_picked_yacddu_vol_p_kernel(
                 in_=x_words[o].rearrange("p n t -> p (n t)").bitcast(I32),
             )
 
-        def load_weight(name, w, o):
-            rows = w[o * K_PASS : (o + 1) * K_PASS, :].rearrange("(p j) c -> p j c", j=PACK)
-            for half in range(2):
-                nc.sync.dma_start(
-                    out=raw[name, o, half][:], in_=rows[:, :, half * (H // 2) : (half + 1) * (H // 2)]
-                )
+        def pass_rows(w, o):
+            return w[o * K_PASS : (o + 1) * K_PASS, :].rearrange("(p j) c -> p j c", j=PACK)
 
-        load_words(0)
-        nc.sync.dma_start(offs_sb[:], offs)
-        for q in range(4):
+        def load_w1(o, half):
             nc.sync.dma_start(
-                out=xs[32 * q : 32 * q + 4 * PASSES, :].bitcast(I32),
+                out=raw["w1", o, half][:],
+                in_=pass_rows(w1, o)[:, :, half * (H // 2) : (half + 1) * (H // 2)],
+            )
+
+        for q in range(4):
+            live = slice(32 * q, 32 * q + 4 * PASSES)
+            nc.sync.dma_start(
+                out=xs_rows[live, :].bitcast(I32),
                 in_=x_scales[:, 4 * q : 4 * q + 4, :].bitcast(I32),
             )
-        load_weight("w1", w1, 0)
+            nc.vector.tensor_copy(xs[live, :].bitcast(I32), xs_rows[live, :].bitcast(I32))
+        nc.sync.dma_start(offs_sb[:], offs)
+        load_words(0)
+        load_w1(0, 0)
+        load_w1(1, 0)
         load_words(1)
-        load_weight("w1", w1, 1)
-        load_weight("w2", w2, 0)
-        load_weight("w2", w2, 1)
-        nc.sync.dma_start(out=raw3[:], in_=w3.rearrange("(p j) n -> p j n", j=PACK))
-        nc.sync.dma_start(out=eps_sb[:], in_=eps.rearrange("(p t) s -> p t s", t=PACK))
-        nc.sync.dma_start(prv_sb[:], prv)
+        load_w1(0, 1)
+        load_w1(1, 1)
         nc.sync.dma_start(out=unit_sb[:], in_=unit.rearrange("(p t) o -> p (t o)", t=PACK))
+        for o in range(PASSES):
+            nc.sync.dma_start(out=raw["w2", o][:], in_=pass_rows(w2, o))
+        nc.sync.dma_start(out=raw3[:], in_=w3.rearrange("(p j) n -> p j n", j=PACK))
+        eps_rows = eps.rearrange("(b p) s -> p b s", p=P)
+        for h in range(2):
+            nc.sync.dma_start(out=eps_sb[:, 2 * h : 2 * h + 2, :], in_=eps_rows[:, 2 * h : 2 * h + 2, :])
+        nc.sync.dma_start(prv_sb[:], prv)
 
         xg = [sb("xg%d" % o, [P, S], U32) for o in range(PASSES)]
         xsg = sb("xsg", [P, S], U8)
@@ -91,32 +104,30 @@ def tile_picked_yacddu_vol_p_kernel(
         def gather_words(o):
             nc.vector.tensor_copy(xg[o][:], xw[o][:].indirect(offs_sb[:]))
 
-        def deal_weight(name, o, sign):
-            grouped = sb("grp_%s_%d" % (name, o), [P, PACK * P * PACK], BF16)
-            view = grouped[:].rearrange("p (t m j) -> p m j t", t=PACK, j=PACK)
-            for half in range(2):
-                src = raw[name, o, half][:].rearrange("p j (m t) -> p m j t", t=PACK)
-                dst = view[:, half * (P // 2) : (half + 1) * (P // 2)]
-                nc.vector.tensor_scalar(dst, src, sign, None, ALU.mult)
-            return grouped
+        def weave_views(name, src):
+            grouped = sb("grp_" + name, [P, PACK * src.shape[2]], BF16)
+            dst = grouped[:].rearrange("p (c i j) -> p c j i", i=4, j=PACK)
+            return grouped, dst, src[:].rearrange("p j (c i) -> p c j i", i=4)
 
-        def quantise_weight(name, o, grouped, pieces):
-            codes = sb("codes_%s_%d" % (name, o), [P, H], U32)
-            scales = sb("scales_%s_%d" % (name, o), [P, H], U8)
-            w = H // pieces
-            for i in range(pieces):
-                nc.vector.quantize_mx(
-                    out=codes[:, i * w : (i + 1) * w].bitcast(FP8X4),
-                    scales=scales[:, i * w : (i + 1) * w],
-                    in_=grouped[:, PACK * i * w : PACK * (i + 1) * w],
-                )
+        def quantise(name, grouped):
+            width = grouped.shape[1] // PACK
+            codes = sb("codes_" + name, [P, width], U32)
+            scales = sb("scales_" + name, [P, width], U8)
+            nc.vector.quantize_mx(out=codes[:].bitcast(FP8X4), scales=scales[:], in_=grouped[:])
             return codes, scales
 
-        def product_pass(banks, o, codes, scales):
-            for t in range(PACK):
-                cols = slice(t * P, (t + 1) * P)
+        def w1_product(o, half):
+            name = "w1_%d_%d" % (o, half)
+            grouped, dst, src = weave_views(name, raw["w1", o, half])
+            if half == 0:
+                nc.scalar.activation(dst, src, ACT.Copy, scale=-1.0)
+            else:
+                nc.vector.tensor_scalar(dst, src, -1.0, None, ALU.mult)
+            codes, scales = quantise(name, grouped)
+            for i in range(2):
+                cols = slice(i * P, (i + 1) * P)
                 nc.tensor.matmul_mx(
-                    out=banks[t][:],
+                    out=neg_y[2 * half + i][:],
                     lhsT=codes[:, cols].bitcast(FP8X4),
                     lhsT_scale=scales[:, cols],
                     rhs=xg[o][:].bitcast(FP8X4),
@@ -125,16 +136,24 @@ def tile_picked_yacddu_vol_p_kernel(
                     stop=(o == PASSES - 1),
                 )
 
-        neg_y = [psum.tile([P, S], F32, name="neg_y%d" % t, tag="bank%d" % t) for t in range(PACK)]
-        vo = [psum.tile([P, S], F32, name="vo%d" % t, tag="bank%d" % (PACK + t)) for t in range(PACK)]
+        def dealt(bank):
+            return bank.rearrange("q (p t) -> q t p", t=PACK)
 
-        gather_words(0)
+        def by_tile(rows):
+            return rows.rearrange("q (t p) -> q t p", t=PACK)
+
+        def turn(dst, src, start, stop):
+            nc.tensor.matmul(dst, lhsT=src, rhs=ident[:], is_transpose=True, start=start, stop=stop)
+
+        neg_y = [psum.tile([P, S], F32, name="neg_y%d" % t, tag="bank%d" % t) for t in range(PACK)]
+
         nc.vector.tensor_copy(xsg[:], xs[:].indirect(offs_sb[:]))
-        c, s = quantise_weight("w1", 0, deal_weight("w1", 0, -1.0), 1)
-        product_pass(neg_y, 0, c, s)
+        gather_words(0)
+        w1_product(0, 0)
         gather_words(1)
-        c, s = quantise_weight("w1", 1, deal_weight("w1", 1, -1.0), PACK)
-        product_pass(neg_y, 1, c, s)
+        w1_product(1, 0)
+        w1_product(0, 1)
+        w1_product(1, 1)
 
         sig_y = sb("sig_y", [P, PACK, S], F32)
         for t in range(PACK):
@@ -142,8 +161,19 @@ def tile_picked_yacddu_vol_p_kernel(
         log_y = sb("log_y", [P, PACK, S], F32)
         nc.scalar.activation(log_y[:], sig_y[:], ACT.Ln, bias=TINY, scale=math.exp(-0.25))
 
+        half_unit = sb("half_unit", [P, PACK], F32)
+        nc.vector.tensor_scalar(half_unit[:], unit_sb[:], -0.5, None, ALU.mult)
+        unit_bank = psum.tile([P, PACK, P], F32, name="unit_bank", tag="bank%d" % (2 * PACK - 1))
+        for t in range(PACK):
+            turn(unit_bank[:, t, :], half_unit[:, t : t + 1].to_broadcast([P, P]), True, True)
+        unit_row = sb("unit_row", [P, H], F32)
+        nc.vector.tensor_copy(unit_row[:], unit_bank[:].rearrange("q t p -> q (t p)"))
+
+        vo = [psum.tile([P, S], F32, name="vo%d" % t, tag="bank%d" % (PACK + t)) for t in range(PACK)]
         for o in range(PASSES):
-            c, s = quantise_weight("w2", o, deal_weight("w2", o, 1.0), 1)
+            grouped, dst, src = weave_views("w2_%d" % o, raw["w2", o])
+            nc.vector.tensor_copy(out=dst, in_=src)
+            c, s = quantise("w2_%d" % o, grouped)
             for ch in range(CHUNKS):
                 cols = slice(ch * P, (ch + 1) * P)
                 nc.tensor.matmul_mx(
@@ -156,23 +186,30 @@ def tile_picked_yacddu_vol_p_kernel(
                     stop=(o == PASSES - 1),
                 )
 
-        grp3 = sb("grp3", [P, N * PACK], BF16)
-        nc.vector.tensor_copy(
-            out=grp3[:].rearrange("p (c i j) -> p c j i", i=4, j=PACK),
-            in_=raw3[:].rearrange("p j (c i) -> p c j i", i=4),
-        )
-        codes3 = sb("codes3", [P, N], U32)
-        scales3 = sb("scales3", [P, N], U8)
-        nc.vector.quantize_mx(out=codes3[:].bitcast(FP8X4), scales=scales3[:], in_=grp3[:])
+        grouped, dst, src = weave_views("w3", raw3)
+        nc.vector.tensor_copy(out=dst, in_=src)
+        codes3, scales3 = quantise("w3", grouped)
 
         for t in range(PACK):
             nc.gpsimd.tensor_scalar(eps_sb[:, t, :], eps_sb[:, t, :], 0.6, 0.0, ALU.mult, ALU.add)
 
         sig_v = sb("sig_v", [P, CHUNKS, H], F32)
-        for ch in range(CHUNKS):
-            nc.scalar.activation(sig_v[:, ch, :], vo[ch][:], ACT.Sigmoid, scale=-1.0)
+        for ch in (2, 3, 0, 1):
+            nc.scalar.activation(by_tile(sig_v[:, ch, :]), dealt(vo[ch][:]), ACT.Sigmoid, scale=-1.0)
         log_v = sb("log_v", [P, CHUNKS, H], F32)
-        nc.scalar.activation(log_v[:], sig_v[:], ACT.Ln, bias=TINY)
+        neg_sp = sb("neg_sp", [P, CHUNKS, H], F32)
+
+        def volume_softplus(first):
+            pair = slice(first, first + 2)
+            nc.scalar.activation(log_v[:, pair, :], sig_v[:, pair, :], ACT.Ln, bias=TINY)
+            return pair
+
+        def clamp_volume(ch):
+            nc.vector.scalar_tensor_tensor(
+                by_tile(neg_sp[:, ch, :]), dealt(vo[ch][:]), -1.0, by_tile(log_v[:, ch, :]), ALU.mult, ALU.min
+            )
+
+        volume_softplus(0)
 
         for t in range(PACK):
             nc.vector.scalar_tensor_tensor(
@@ -188,10 +225,9 @@ def tile_picked_yacddu_vol_p_kernel(
                     ALU.mult,
                 )
 
-        def turn(dst, src, start, stop):
-            nc.tensor.matmul(dst, lhsT=src, rhs=ident[:], is_transpose=True, start=start, stop=stop)
-
-        log_dur = sig_v
+        clamp_volume(0)
+        clamp_volume(1)
+        log_dur = sb("log_dur", [P, CHUNKS, H], F32)
         log_psin = sb("log_psin", [P, CHUNKS, H], F32)
         for ch in range(CHUNKS):
             cols = slice(ch * P, (ch + 1) * P)
@@ -200,57 +236,65 @@ def tile_picked_yacddu_vol_p_kernel(
             dur_t = psum.tile([P, PACK, P], F32, name="dur_t%d" % ch, tag="bank%d" % (2 * within))
             psin_t = psum.tile([P, PACK, P], F32, name="psin_t%d" % ch, tag="bank%d" % (2 * within + 1))
             for t in range(PACK):
-                turn(psin_t[:, t, :], neg_s[t][:, cols], t == 0, False)
-            for t in range(PACK):
                 turn(dur_t[:, t, :], neg_d[h][:, t, part], True, True)
+            for t in range(PACK):
+                turn(psin_t[:, t, :], neg_s[t][:, cols], t == 0, False)
             for t in range(PACK):
                 turn(psin_t[:, t, :], neg_d[h][:, t, part], False, t == PACK - 1)
             nc.scalar.activation(
-                log_dur[:, ch, :], dur_t[:].rearrange("p t c -> p (t c)"), ACT.Ln, bias=TINY, scale=-0.8 / 0.6
+                by_tile(log_dur[:, ch, :]), dealt(dur_t[:].rearrange("q b p -> q (b p)")), ACT.Ln, bias=TINY, scale=-0.8 / 0.6
             )
             nc.scalar.activation(
-                log_psin[:, ch, :], psin_t[:].rearrange("p t c -> p (t c)"), ACT.Ln, bias=0.1, scale=-0.4
+                by_tile(log_psin[:, ch, :]), dealt(psin_t[:].rearrange("q b p -> q (b p)")), ACT.Ln, bias=0.1, scale=-0.4
             )
+            if ch == 1:
+                volume_softplus(2)
+                clamp_volume(2)
+                clamp_volume(3)
 
-        neg_sp = sb("neg_sp", [P, CHUNKS, H], F32)
-        for ch in range(CHUNKS):
-            nc.vector.scalar_tensor_tensor(
-                neg_sp[:, ch, :], vo[ch][:], -1.0, log_v[:, ch, :], ALU.mult, ALU.min
-            )
         log_haz = sb("log_haz", [P, CHUNKS, H], F32)
         for chs in (slice(0, 1), slice(1, 2), slice(2, 4)):
             nc.vector.scalar_tensor_tensor(
                 log_haz[:, chs, :], log_dur[:, chs, :], 0.5, log_psin[:, chs, :], ALU.mult, ALU.subtract
             )
-        half_unit = sb("half_unit", [P, PACK], F32)
-        nc.vector.tensor_scalar(half_unit[:], unit_sb[:], -0.5, None, ALU.mult)
+        scaled = {}
+        for ch in ON_SCALAR:
+            sp_u = sb("sp_u%d" % ch, [P, H], F32)
+            nc.vector.tensor_tensor(sp_u[:], neg_sp[:, ch, :], unit_row[:], ALU.mult)
+            psin_u = sb("psin_u%d" % ch, [P, H], F32)
+            nc.vector.tensor_tensor(psin_u[:], log_psin[:, ch, :], unit_row[:], ALU.mult)
+            scaled[ch] = (sp_u[:], psin_u[:])
 
         out_view = out.rearrange("(a p) s -> p a s", p=P)
         ratio = [log_dur[:, (ch + 2) % CHUNKS, :] for ch in range(CHUNKS)]
         for ch in range(CHUNKS):
             nc.scalar.activation(ratio[ch], log_haz[:, ch, :], ACT.Sigmoid, bias=-math.log(0.7))
+        totals = []
         for ch in range(CHUNKS):
-            cols = slice(ch * P, (ch + 1) * P)
+            sp_term, psin_term = scaled.get(ch, (neg_sp[:, ch, :], log_psin[:, ch, :]))
             neg_vol = sb("neg_vol%d" % ch, [P, H], F32)
-            nc.vector.scalar_tensor_tensor(
-                neg_vol[:], neg_sp[:, ch, :], 2.0, ratio[ch], ALU.mult, ALU.mult
-            )
-            total = psum.tile([P, PACK, P], F32, name="total%d" % ch, tag="bank%d" % (PACK + ch))
+            nc.vector.scalar_tensor_tensor(neg_vol[:], sp_term, 2.0, ratio[ch], ALU.mult, ALU.mult)
+            total = psum.tile([P, PACK, P], F32, name="total%d" % ch, tag="bank%d" % ch)
             for t in range(PACK):
-                turn(total[:, t, :], log_psin[:, ch, t * P : (t + 1) * P], t == 0, False)
+                turn(total[:, t, :], psin_term[:, t * P : (t + 1) * P], t == 0, False)
             for t in range(PACK):
                 turn(total[:, t, :], neg_vol[:, t * P : (t + 1) * P], False, t == PACK - 1)
+            totals.append(total)
+        for ch in range(CHUNKS):
+            cols = slice(ch * P, (ch + 1) * P)
             hid_grp = sb("hid_grp%d" % ch, [P, P * PACK], BF16)
-            nc.vector.tensor_tensor(
-                hid_grp[:].rearrange("p (c t) -> p c t", t=PACK),
-                total[:].rearrange("p t c -> p c t"),
-                half_unit[:].unsqueeze(1).to_broadcast([P, P, PACK]),
-                ALU.mult,
-            )
+            woven = hid_grp[:].rearrange("p (c t) -> p c t", t=PACK)
+            planes = totals[ch][:].rearrange("p t c -> p c t")
+            if ch in scaled:
+                nc.scalar.copy(out=woven, in_=planes)
+            else:
+                nc.vector.tensor_tensor(
+                    woven, planes, half_unit[:].unsqueeze(1).to_broadcast([P, P, PACK]), ALU.mult
+                )
             hid_codes = sb("hid_codes%d" % ch, [P, P], U32)
             hid_scales = sb("hid_scales%d" % ch, [P, P], U8)
             nc.vector.quantize_mx(out=hid_codes[:].bitcast(FP8X4), scales=hid_scales[:], in_=hid_grp[:])
-            acc = psum.tile([P, N // P, P], F32, name="acc%d" % ch, tag="bank%d" % ch)
+            acc = psum.tile([P, N // P, P], F32, name="acc%d" % ch, tag="bank%d" % (PACK + ch))
             for a in range(N // P):
                 nc.tensor.matmul_mx(
                     out=acc[:, a, :],

@@ -25,6 +25,7 @@ TINY = 2.0 ** -60
 CHUNKS = S // P
 HALF = S // 2
 ON_SCALAR = (0, 2)
+W1_PIECES = ((0, 0, 2), (1, 0, 2), (0, 2, 2), (1, 2, 1), (1, 3, 1))
 
 
 def tile_picked_yacddu_vol_p_kernel(
@@ -36,7 +37,7 @@ def tile_picked_yacddu_vol_p_kernel(
         psum = ctx.enter_context(tc.psum_pool(name="psum", bufs=1))
 
         def sb(name, shape, dtype):
-            return keep.tile(shape, dtype, name=name, align_bytes=64)
+            return keep.tile(shape, dtype, name=name, tag=name, align_bytes=64)
 
         offs_sb = keep.tile([P, S // 16], U16, name="offs_sb")
         prv_sb = keep.tile([P, S // 16], U16, name="prv_sb")
@@ -45,13 +46,12 @@ def tile_picked_yacddu_vol_p_kernel(
         xs = sb("xs", [P, T], U8)
         raw = {}
         for o in range(PASSES):
-            for half in range(2):
-                raw["w1", o, half] = sb("raw_w1_%d_%d" % (o, half), [P, PACK, H // 2], F32)
             raw["w2", o] = sb("raw_w2_%d" % o, [P, PACK, H], F32)
+        for o, first, blocks in W1_PIECES:
+            raw["w1", o, first] = sb("raw_w1_%d_%d" % (o, first), [P, PACK, blocks * P], F32)
         raw3 = sb("raw3", [P, PACK, N], F32)
         eps_sb = sb("eps_sb", [P, PACK, S], F32)
         unit_sb = sb("unit_sb", [P, PACK], F32)
-        neg_s = [sb("neg_s%d" % t, [P, S], F32) for t in range(PACK)]
 
         nc.vector.memset(xs[:].bitcast(I32), 0)
         warm = sb("warm", [P, 2], F32)
@@ -69,10 +69,9 @@ def tile_picked_yacddu_vol_p_kernel(
         def pass_rows(w, o):
             return w[o * K_PASS : (o + 1) * K_PASS, :].rearrange("(p j) c -> p j c", j=PACK)
 
-        def load_w1(o, half):
+        def load_w1(o, first, blocks):
             nc.sync.dma_start(
-                out=raw["w1", o, half][:],
-                in_=pass_rows(w1, o)[:, :, half * (H // 2) : (half + 1) * (H // 2)],
+                out=raw["w1", o, first][:], in_=pass_rows(w1, o)[:, :, first * P : (first + blocks) * P]
             )
 
         for q in range(4):
@@ -84,19 +83,19 @@ def tile_picked_yacddu_vol_p_kernel(
             nc.vector.tensor_copy(xs[live, :].bitcast(I32), xs_rows[live, :].bitcast(I32))
         nc.sync.dma_start(offs_sb[:], offs)
         load_words(0)
-        load_w1(0, 0)
-        load_w1(1, 0)
-        load_words(1)
-        load_w1(0, 1)
-        load_w1(1, 1)
+        load_w1(*W1_PIECES[0])
         nc.sync.dma_start(out=unit_sb[:], in_=unit.rearrange("(p t) o -> p (t o)", t=PACK))
+        load_w1(*W1_PIECES[1])
+        load_words(1)
+        for piece in W1_PIECES[2:]:
+            load_w1(*piece)
         for o in range(PASSES):
             nc.sync.dma_start(out=raw["w2", o][:], in_=pass_rows(w2, o))
-        nc.sync.dma_start(out=raw3[:], in_=w3.rearrange("(p j) n -> p j n", j=PACK))
         eps_rows = eps.rearrange("(b p) s -> p b s", p=P)
-        for h in range(2):
+        for h in (1, 0):
             nc.sync.dma_start(out=eps_sb[:, 2 * h : 2 * h + 2, :], in_=eps_rows[:, 2 * h : 2 * h + 2, :])
         nc.sync.dma_start(prv_sb[:], prv)
+        nc.sync.dma_start(out=raw3[:], in_=w3.rearrange("(p j) n -> p j n", j=PACK))
 
         xg = [sb("xg%d" % o, [P, S], U32) for o in range(PASSES)]
         xsg = sb("xsg", [P, S], U8)
@@ -116,18 +115,18 @@ def tile_picked_yacddu_vol_p_kernel(
             nc.vector.quantize_mx(out=codes[:].bitcast(FP8X4), scales=scales[:], in_=grouped[:])
             return codes, scales
 
-        def w1_product(o, half):
-            name = "w1_%d_%d" % (o, half)
-            grouped, dst, src = weave_views(name, raw["w1", o, half])
-            if half == 0:
+        def w1_product(o, first, blocks):
+            name = "w1_%d_%d" % (o, first)
+            grouped, dst, src = weave_views(name, raw["w1", o, first])
+            if first == 0:
                 nc.scalar.activation(dst, src, ACT.Copy, scale=-1.0)
             else:
                 nc.vector.tensor_scalar(dst, src, -1.0, None, ALU.mult)
             codes, scales = quantise(name, grouped)
-            for i in range(2):
+            for i in range(blocks):
                 cols = slice(i * P, (i + 1) * P)
                 nc.tensor.matmul_mx(
-                    out=neg_y[2 * half + i][:],
+                    out=neg_y[first + i][:],
                     lhsT=codes[:, cols].bitcast(FP8X4),
                     lhsT_scale=scales[:, cols],
                     rhs=xg[o][:].bitcast(FP8X4),
@@ -149,32 +148,41 @@ def tile_picked_yacddu_vol_p_kernel(
 
         nc.vector.tensor_copy(xsg[:], xs[:].indirect(offs_sb[:]))
         gather_words(0)
-        w1_product(0, 0)
+        w1_product(*W1_PIECES[0])
         gather_words(1)
-        w1_product(1, 0)
-        w1_product(0, 1)
-        w1_product(1, 1)
-
-        sig_y = sb("sig_y", [P, PACK, S], F32)
-        for t in range(PACK):
-            nc.scalar.activation(sig_y[:, t, :], neg_y[t][:], ACT.Sigmoid)
-        log_y = sb("log_y", [P, PACK, S], F32)
-        nc.scalar.activation(log_y[:], sig_y[:], ACT.Ln, bias=TINY, scale=math.exp(-0.25))
-
+        w1_product(*W1_PIECES[1])
         half_unit = sb("half_unit", [P, PACK], F32)
-        nc.vector.tensor_scalar(half_unit[:], unit_sb[:], -0.5, None, ALU.mult)
+        nc.gpsimd.tensor_scalar(half_unit[:], unit_sb[:], -0.5, 0.0, ALU.mult, ALU.add)
         unit_bank = psum.tile([P, PACK, P], F32, name="unit_bank", tag="bank%d" % (2 * PACK - 1))
         for t in range(PACK):
             turn(unit_bank[:, t, :], half_unit[:, t : t + 1].to_broadcast([P, P]), True, True)
         unit_row = sb("unit_row", [P, H], F32)
-        nc.vector.tensor_copy(unit_row[:], unit_bank[:].rearrange("q t p -> q (t p)"))
+        nc.scalar.copy(unit_row[:], unit_bank[:].rearrange("q t p -> q (t p)"))
+
+        for piece in W1_PIECES[2:]:
+            w1_product(*piece)
+
+        sig_y = sb("sig_y", [P, PACK, S], F32)
+        for t in range(PACK):
+            nc.scalar.activation(sig_y[:, t, :], neg_y[t][:], ACT.Sigmoid)
+        log_high = sb("log_high", [P, 2, S], F32)
+        nc.scalar.activation(log_high[:], sig_y[:, 2:4, :], ACT.Ln, bias=TINY, scale=math.exp(-0.25))
+        nc.scalar.activation(sig_y[:, 2:4, :], sig_y[:, 0:2, :], ACT.Ln, bias=TINY, scale=math.exp(-0.25))
+        log_y = [sig_y[:, 2, :], sig_y[:, 3, :], log_high[:, 0, :], log_high[:, 1, :]]
 
         vo = [psum.tile([P, S], F32, name="vo%d" % t, tag="bank%d" % (PACK + t)) for t in range(PACK)]
         for o in range(PASSES):
-            grouped, dst, src = weave_views("w2_%d" % o, raw["w2", o])
-            nc.vector.tensor_copy(out=dst, in_=src)
-            c, s = quantise("w2_%d" % o, grouped)
-            for ch in range(CHUNKS):
+            c = sb("codes_w2_%d" % o, [P, H], U32)
+            s = sb("scales_w2_%d" % o, [P, H], U8)
+            halves = []
+            for h in range(2):
+                cols = slice(h * (H // 2), (h + 1) * (H // 2))
+                grouped, dst, src = weave_views("w2_%d_%d" % (o, h), raw["w2", o][:, :, cols])
+                nc.vector.tensor_copy(out=dst, in_=src)
+                halves.append((grouped, cols))
+            for grouped, cols in halves:
+                nc.vector.quantize_mx(out=c[:, cols].bitcast(FP8X4), scales=s[:, cols], in_=grouped[:])
+            for ch in (2, 3, 0, 1):
                 cols = slice(ch * P, (ch + 1) * P)
                 nc.tensor.matmul_mx(
                     out=vo[ch][:],
@@ -186,12 +194,10 @@ def tile_picked_yacddu_vol_p_kernel(
                     stop=(o == PASSES - 1),
                 )
 
-        grouped, dst, src = weave_views("w3", raw3)
-        nc.vector.tensor_copy(out=dst, in_=src)
-        codes3, scales3 = quantise("w3", grouped)
-
-        for t in range(PACK):
-            nc.gpsimd.tensor_scalar(eps_sb[:, t, :], eps_sb[:, t, :], 0.6, 0.0, ALU.mult, ALU.add)
+        eps_first = sb("grp_w2_1_1", [P, S], F32)
+        eps_scaled = {2: eps_first[:], 3: eps_sb[:, 2, :], 0: eps_sb[:, 3, :], 1: eps_sb[:, 0, :]}
+        for t in (2, 3, 0, 1):
+            nc.gpsimd.tensor_scalar(eps_scaled[t], eps_sb[:, t, :], 0.6, 0.0, ALU.mult, ALU.add)
 
         sig_v = sb("sig_v", [P, CHUNKS, H], F32)
         for ch in (2, 3, 0, 1):
@@ -211,19 +217,31 @@ def tile_picked_yacddu_vol_p_kernel(
 
         volume_softplus(0)
 
-        for t in range(PACK):
+        neg_s = [sb("grp_w2_1_0" if t == 2 else "neg_s%d" % t, [P, S], F32) for t in range(PACK)]
+        for t in (2, 3, 0, 1):
             nc.vector.scalar_tensor_tensor(
-                neg_s[t][:], neg_y[t][:], -0.25, log_y[:, t, :], ALU.add, ALU.min
+                neg_s[t][:], neg_y[t][:], -0.25, log_y[t], ALU.add, ALU.min
             )
+        def open_psin(ch):
+            bank = psum.tile([P, PACK, P], F32, name="psin_t%d" % ch, tag="bank%d" % (2 * (ch % 2) + 1))
+            for t in range(PACK):
+                turn(bank[:, t, :], neg_s[t][:, ch * P : (ch + 1) * P], t == 0, False)
+            return bank
+
+        early = [open_psin(ch) for ch in range(2)]
         neg_d = [sb("neg_d%d" % h, [P, PACK, HALF], F32) for h in range(2)]
         for h in range(2):
-            for t in range(PACK):
+            for t in (2, 3, 0, 1):
                 nc.vector.tensor_tensor(
                     neg_d[h][:, t, :],
                     neg_s[t][:].indirect(prv_sb[:, h * (HALF // 16) : (h + 1) * (HALF // 16)]),
-                    eps_sb[:, t, h * HALF : (h + 1) * HALF],
+                    eps_scaled[t][:, h * HALF : (h + 1) * HALF],
                     ALU.mult,
                 )
+
+        grouped, dst, src = weave_views("w3", raw3)
+        nc.vector.tensor_copy(out=dst, in_=src)
+        codes3, scales3 = quantise("w3", grouped)
 
         clamp_volume(0)
         clamp_volume(1)
@@ -234,11 +252,12 @@ def tile_picked_yacddu_vol_p_kernel(
             h, within = divmod(ch, 2)
             part = slice(within * P, (within + 1) * P)
             dur_t = psum.tile([P, PACK, P], F32, name="dur_t%d" % ch, tag="bank%d" % (2 * within))
-            psin_t = psum.tile([P, PACK, P], F32, name="psin_t%d" % ch, tag="bank%d" % (2 * within + 1))
+            if h == 0:
+                psin_t = early[ch]
             for t in range(PACK):
                 turn(dur_t[:, t, :], neg_d[h][:, t, part], True, True)
-            for t in range(PACK):
-                turn(psin_t[:, t, :], neg_s[t][:, cols], t == 0, False)
+            if h == 1:
+                psin_t = open_psin(ch)
             for t in range(PACK):
                 turn(psin_t[:, t, :], neg_d[h][:, t, part], False, t == PACK - 1)
             nc.scalar.activation(

@@ -54,9 +54,6 @@ def tile_picked_yacddu_vol_p_kernel(
         unit_sb = sb("unit_sb", [P, PACK], F32)
 
         nc.vector.memset(xs[:].bitcast(I32), 0)
-        warm = sb("warm", [P, 2], F32)
-        nc.gpsimd.memset(warm[:, 0:1], 0.0)
-        nc.scalar.activation(warm[:, 1:2], warm[:, 0:1], ACT.Sigmoid)
         ident = sb("ident", [P, P], F32)
         make_identity(nc, ident[:])
 

import math
from contextlib import ExitStack

import concourse.mybir as mybir
from concourse.masks import make_identity

K, T, S, N, H = 1024, 1024, 512, 256, 512
FLOPS = 2 * K * H * S * 2 + 2 * H * N * S

F32 = mybir.dt.float32
BF16 = mybir.dt.bfloat16
I32 = mybir.dt.int32
U32 = mybir.dt.uint32
U16 = mybir.dt.uint16
U8 = mybir.dt.uint8
FP8X4 = mybir.dt.float8_e4m3fn_x4
ALU = mybir.AluOpType
ACT = mybir.ActivationFunctionType

P = 128
PACK = 4
K_PASS = P * PACK
PASSES = K // K_PASS
TINY = 2.0 ** -60
CHUNKS = S // P
HALF = S // 2
ON_SCALAR = (0, 2)
W1_PIECES = ((0, 0, 2), (1, 0, 2), (0, 2, 2), (1, 2, 1), (1, 3, 1))


def tile_picked_yacddu_vol_p_kernel(
    tc, x_words, x_scales, w1, w2, eps, unit, w3, offs, prv, out
):
    nc = tc.nc
    with ExitStack() as ctx:
        keep = ctx.enter_context(tc.tile_pool(name="keep", bufs=1))
        psum = ctx.enter_context(tc.psum_pool(name="psum", bufs=1))

        def sb(name, shape, dtype):
            return keep.tile(shape, dtype, name=name, tag=name, align_bytes=64)

        offs_sb = keep.tile([P, S // 16], U16, name="offs_sb")
        prv_sb = keep.tile([P, S // 16], U16, name="prv_sb")
        xw = [sb("xw%d" % o, [P, T], U32) for o in range(PASSES)]
        xs_rows = sb("xs_rows", [P, T], U8)
        xs = sb("xs", [P, T], U8)
        raw = {}
        for o in range(PASSES):
            raw["w2", o] = sb("raw_w2_%d" % o, [P, PACK, H], F32)
        for o, first, blocks in W1_PIECES:
            raw["w1", o, first] = sb("raw_w1_%d_%d" % (o, first), [P, PACK, blocks * P], F32)
        raw3 = sb("raw3", [P, PACK, N], F32)
        eps_sb = sb("eps_sb", [P, PACK, S], F32)
        unit_sb = sb("unit_sb", [P, PACK], F32)

        nc.vector.memset(xs[:].bitcast(I32), 0)
        ident = sb("ident", [P, P], F32)
        make_identity(nc, ident[:])

        def load_words(o):
            nc.sync.dma_start(
                out=xw[o][:].bitcast(I32),
                in_=x_words[o].rearrange("p n t -> p (n t)").bitcast(I32),
            )

        def pass_rows(w, o):
            return w[o * K_PASS : (o + 1) * K_PASS, :].rearrange("(p j) c -> p j c", j=PACK)

        def load_w1(o, first, blocks):
            nc.sync.dma_start(
                out=raw["w1", o, first][:], in_=pass_rows(w1, o)[:, :, first * P : (first + blocks) * P]
            )

        for q in range(4):
            live = slice(32 * q, 32 * q + 4 * PASSES)
            nc.sync.dma_start(
                out=xs_rows[live, :].bitcast(I32),
                in_=x_scales[:, 4 * q : 4 * q + 4, :].bitcast(I32),
            )
            nc.vector.tensor_copy(xs[live, :].bitcast(I32), xs_rows[live, :].bitcast(I32))
        nc.sync.dma_start(offs_sb[:], offs)
        load_words(0)
        load_w1(*W1_PIECES[0])
        nc.sync.dma_start(out=unit_sb[:], in_=unit.rearrange("(p t) o -> p (t o)", t=PACK))
        load_w1(*W1_PIECES[1])
        load_words(1)
        for piece in W1_PIECES[2:]:
            load_w1(*piece)
        for o in range(PASSES):
            nc.sync.dma_start(out=raw["w2", o][:], in_=pass_rows(w2, o))
        eps_rows = eps.rearrange("(b p) s -> p b s", p=P)
        for h in (1, 0):
            nc.sync.dma_start(out=eps_sb[:, 2 * h : 2 * h + 2, :], in_=eps_rows[:, 2 * h : 2 * h + 2, :])
        nc.sync.dma_start(prv_sb[:], prv)
        nc.sync.dma_start(out=raw3[:], in_=w3.rearrange("(p j) n -> p j n", j=PACK))

        xg = [sb("xg%d" % o, [P, S], U32) for o in range(PASSES)]
        xsg = sb("xsg", [P, S], U8)

        def gather_words(o):
            nc.vector.tensor_copy(xg[o][:], xw[o][:].indirect(offs_sb[:]))

        def weave_views(name, src):
            grouped = sb("grp_" + name, [P, PACK * src.shape[2]], BF16)
            dst = grouped[:].rearrange("p (c i j) -> p c j i", i=4, j=PACK)
            return grouped, dst, src[:].rearrange("p j (c i) -> p c j i", i=4)

        def quantise(name, grouped):
            width = grouped.shape[1] // PACK
            codes = sb("codes_" + name, [P, width], U32)
            scales = sb("scales_" + name, [P, width], U8)
            nc.vector.quantize_mx(out=codes[:].bitcast(FP8X4), scales=scales[:], in_=grouped[:])
            return codes, scales

        def w1_product(o, first, blocks):
            name = "w1_%d_%d" % (o, first)
            grouped, dst, src = weave_views(name, raw["w1", o, first])
            if first == 0:
                nc.scalar.activation(dst, src, ACT.Copy, scale=-1.0)
            else:
                nc.vector.tensor_scalar(dst, src, -1.0, None, ALU.mult)
            codes, scales = quantise(name, grouped)
            for i in range(blocks):
                cols = slice(i * P, (i + 1) * P)
                nc.tensor.matmul_mx(
                    out=neg_y[first + i][:],
                    lhsT=codes[:, cols].bitcast(FP8X4),
                    lhsT_scale=scales[:, cols],
                    rhs=xg[o][:].bitcast(FP8X4),
                    rhs_scale=xsg[4 * o : P, :],
                    start=(o == 0),
                    stop=(o == PASSES - 1),
                )

        def dealt(bank):
            return bank.rearrange("q (p t) -> q t p", t=PACK)

        def by_tile(rows):
            return rows.rearrange("q (t p) -> q t p", t=PACK)

        def turn(dst, src, start, stop):
            nc.tensor.matmul(dst, lhsT=src, rhs=ident[:], is_transpose=True, start=start, stop=stop)

        neg_y = [psum.tile([P, S], F32, name="neg_y%d" % t, tag="bank%d" % t) for t in range(PACK)]

        nc.vector.tensor_copy(xsg[:], xs[:].indirect(offs_sb[:]))
        gather_words(0)
        w1_product(*W1_PIECES[0])
        gather_words(1)
        w1_product(*W1_PIECES[1])
        half_unit = sb("half_unit", [P, PACK], F32)
        nc.gpsimd.tensor_scalar(half_unit[:], unit_sb[:], -0.5, 0.0, ALU.mult, ALU.add)
        unit_bank = psum.tile([P, PACK, P], F32, name="unit_bank", tag="bank%d" % (2 * PACK - 1))
        for t in range(PACK):
            turn(unit_bank[:, t, :], half_unit[:, t : t + 1].to_broadcast([P, P]), True, True)
        unit_row = sb("unit_row", [P, H], F32)
        nc.scalar.copy(unit_row[:], unit_bank[:].rearrange("q t p -> q (t p)"))

        for piece in W1_PIECES[2:]:
            w1_product(*piece)

        sig_y = sb("sig_y", [P, PACK, S], F32)
        for t in range(PACK):
            nc.scalar.activation(sig_y[:, t, :], neg_y[t][:], ACT.Sigmoid)
        log_high = sb("log_high", [P, 2, S], F32)
        nc.scalar.activation(log_high[:], sig_y[:, 2:4, :], ACT.Ln, bias=TINY, scale=math.exp(-0.25))
        nc.scalar.activation(sig_y[:, 2:4, :], sig_y[:, 0:2, :], ACT.Ln, bias=TINY, scale=math.exp(-0.25))
        log_y = [sig_y[:, 2, :], sig_y[:, 3, :], log_high[:, 0, :], log_high[:, 1, :]]

        vo = [psum.tile([P, S], F32, name="vo%d" % t, tag="bank%d" % (PACK + t)) for t in range(PACK)]
        for o in range(PASSES):
            c = sb("codes_w2_%d" % o, [P, H], U32)
            s = sb("scales_w2_%d" % o, [P, H], U8)
            halves = []
            for h in range(2):
                cols = slice(h * (H // 2), (h + 1) * (H // 2))
                grouped, dst, src = weave_views("w2_%d_%d" % (o, h), raw["w2", o][:, :, cols])
                nc.vector.tensor_copy(out=dst, in_=src)
                halves.append((grouped, cols))
            for grouped, cols in halves:
                nc.vector.quantize_mx(out=c[:, cols].bitcast(FP8X4), scales=s[:, cols], in_=grouped[:])
            for ch in (2, 3, 0, 1):
                cols = slice(ch * P, (ch + 1) * P)
                nc.tensor.matmul_mx(
                    out=vo[ch][:],
                    lhsT=xg[o][:, cols].bitcast(FP8X4),
                    lhsT_scale=xsg[4 * o : P, cols],
                    rhs=c[:].bitcast(FP8X4),
                    rhs_scale=s[:],
                    start=(o == 0),
                    stop=(o == PASSES - 1),
                )

        eps_first = sb("grp_w2_1_1", [P, S], F32)
        eps_scaled = {2: eps_first[:], 3: eps_sb[:, 2, :], 0: eps_sb[:, 3, :], 1: eps_sb[:, 0, :]}
        for t in (2, 3, 0, 1):
            nc.gpsimd.tensor_scalar(eps_scaled[t], eps_sb[:, t, :], 0.6, 0.0, ALU.mult, ALU.add)

        sig_v = sb("sig_v", [P, CHUNKS, H], F32)
        for ch in (2, 3, 0, 1):
            nc.scalar.activation(by_tile(sig_v[:, ch, :]), dealt(vo[ch][:]), ACT.Sigmoid, scale=-1.0)
        log_v = sb("log_v", [P, CHUNKS, H], F32)
        neg_sp = sb("neg_sp", [P, CHUNKS, H], F32)

        def volume_softplus(first):
            pair = slice(first, first + 2)
            nc.scalar.activation(log_v[:, pair, :], sig_v[:, pair, :], ACT.Ln, bias=TINY)
            return pair

        def clamp_volume(ch):
            nc.vector.scalar_tensor_tensor(
                by_tile(neg_sp[:, ch, :]), dealt(vo[ch][:]), -1.0, by_tile(log_v[:, ch, :]), ALU.mult, ALU.min
            )

        volume_softplus(0)

        neg_s = [sb("grp_w2_1_0" if t == 2 else "neg_s%d" % t, [P, S], F32) for t in range(PACK)]
        for t in (2, 3, 0, 1):
            nc.vector.scalar_tensor_tensor(
                neg_s[t][:], neg_y[t][:], -0.25, log_y[t], ALU.add, ALU.min
            )
        def open_psin(ch):
            bank = psum.tile([P, PACK, P], F32, name="psin_t%d" % ch, tag="bank%d" % (2 * (ch % 2) + 1))
            for t in range(PACK):
                turn(bank[:, t, :], neg_s[t][:, ch * P : (ch + 1) * P], t == 0, False)
            return bank

        early = [open_psin(ch) for ch in range(2)]
        neg_d = [sb("neg_d%d" % h, [P, PACK, HALF], F32) for h in range(2)]
        for h in range(2):
            for t in (2, 3, 0, 1):
                nc.vector.tensor_tensor(
                    neg_d[h][:, t, :],
                    neg_s[t][:].indirect(prv_sb[:, h * (HALF // 16) : (h + 1) * (HALF // 16)]),
                    eps_scaled[t][:, h * HALF : (h + 1) * HALF],
                    ALU.mult,
                )

        grouped, dst, src = weave_views("w3", raw3)
        nc.vector.tensor_copy(out=dst, in_=src)
        codes3, scales3 = quantise("w3", grouped)

        clamp_volume(0)
        clamp_volume(1)
        log_dur = sb("log_dur", [P, CHUNKS, H], F32)
        log_psin = sb("log_psin", [P, CHUNKS, H], F32)
        for ch in range(CHUNKS):
            cols = slice(ch * P, (ch + 1) * P)
            h, within = divmod(ch, 2)
            part = slice(within * P, (within + 1) * P)
            dur_t = psum.tile([P, PACK, P], F32, name="dur_t%d" % ch, tag="bank%d" % (2 * within))
            if h == 0:
                psin_t = early[ch]
            for t in range(PACK):
                turn(dur_t[:, t, :], neg_d[h][:, t, part], True, True)
            if h == 1:
                psin_t = open_psin(ch)
            for t in range(PACK):
                turn(psin_t[:, t, :], neg_d[h][:, t, part], False, t == PACK - 1)
            nc.scalar.activation(
                by_tile(log_dur[:, ch, :]), dealt(dur_t[:].rearrange("q b p -> q (b p)")), ACT.Ln, bias=TINY, scale=-0.8 / 0.6
            )
            nc.scalar.activation(
                by_tile(log_psin[:, ch, :]), dealt(psin_t[:].rearrange("q b p -> q (b p)")), ACT.Ln, bias=0.1, scale=-0.4
            )
            if ch == 1:
                volume_softplus(2)
                clamp_volume(2)
                clamp_volume(3)

        log_haz = sb("log_haz", [P, CHUNKS, H], F32)
        for chs in (slice(0, 1), slice(1, 2), slice(2, 4)):
            nc.vector.scalar_tensor_tensor(
                log_haz[:, chs, :], log_dur[:, chs, :], 0.5, log_psin[:, chs, :], ALU.mult, ALU.subtract
            )
        scaled = {}
        for ch in ON_SCALAR:
            sp_u = sb("sp_u%d" % ch, [P, H], F32)
            nc.vector.tensor_tensor(sp_u[:], neg_sp[:, ch, :], unit_row[:], ALU.mult)
            psin_u = sb("psin_u%d" % ch, [P, H], F32)
            nc.vector.tensor_tensor(psin_u[:], log_psin[:, ch, :], unit_row[:], ALU.mult)
            scaled[ch] = (sp_u[:], psin_u[:])

        out_view = out.rearrange("(a p) s -> p a s", p=P)
        ratio = [log_dur[:, (ch + 2) % CHUNKS, :] for ch in range(CHUNKS)]
        for ch in range(CHUNKS):
            nc.scalar.activation(ratio[ch], log_haz[:, ch, :], ACT.Sigmoid, bias=-math.log(0.7))
        totals = []
        for ch in range(CHUNKS):
            sp_term, psin_term = scaled.get(ch, (neg_sp[:, ch, :], log_psin[:, ch, :]))
            neg_vol = sb("neg_vol%d" % ch, [P, H], F32)
            nc.vector.scalar_tensor_tensor(neg_vol[:], sp_term, 2.0, ratio[ch], ALU.mult, ALU.mult)
            total = psum.tile([P, PACK, P], F32, name="total%d" % ch, tag="bank%d" % ch)
            for t in range(PACK):
                turn(total[:, t, :], psin_term[:, t * P : (t + 1) * P], t == 0, False)
            for t in range(PACK):
                turn(total[:, t, :], neg_vol[:, t * P : (t + 1) * P], False, t == PACK - 1)
            totals.append(total)
        for ch in range(CHUNKS):
            cols = slice(ch * P, (ch + 1) * P)
            hid_grp = sb("hid_grp%d" % ch, [P, P * PACK], BF16)
            woven = hid_grp[:].rearrange("p (c t) -> p c t", t=PACK)
            planes = totals[ch][:].rearrange("p t c -> p c t")
            if ch in scaled:
                nc.scalar.copy(out=woven, in_=planes)
            else:
                nc.vector.tensor_tensor(
                    woven, planes, half_unit[:].unsqueeze(1).to_broadcast([P, P, PACK]), ALU.mult
                )
            hid_codes = sb("hid_codes%d" % ch, [P, P], U32)
            hid_scales = sb("hid_scales%d" % ch, [P, P], U8)
            nc.vector.quantize_mx(out=hid_codes[:].bitcast(FP8X4), scales=hid_scales[:], in_=hid_grp[:])
            acc = psum.tile([P, N // P, P], F32, name="acc%d" % ch, tag="bank%d" % (PACK + ch))
            for a in range(N // P):
                nc.tensor.matmul_mx(
                    out=acc[:, a, :],
                    lhsT=codes3[:, a * P : (a + 1) * P].bitcast(FP8X4),
                    lhsT_scale=scales3[:, a * P : (a + 1) * P],
                    rhs=hid_codes[:].bitcast(FP8X4),
                    rhs_scale=hid_scales[:],
                    start=True,
                    stop=True,
                )
            res = sb("res%d" % ch, [P, N // P, P], F32)
            nc.scalar.copy(out=res[:], in_=acc[:])
            nc.sync.dma_start(out=out_view[:, :, cols], in_=res[:])
